import numpy as np
import ml_dtypes


def mxq(x, axis, fmt="e4m3"):
    dtype, down = {"e4m3": (ml_dtypes.float8_e4m3fn, 7), "e5m2": (ml_dtypes.float8_e5m2, 14)}[fmt]
    v = np.moveaxis(np.asarray(x, np.float32).astype(ml_dtypes.bfloat16).astype(np.float64), axis, -1)
    blocks = v.reshape(v.shape[:-1] + (-1, 32))
    amax = np.abs(blocks).max(-1, keepdims=True)
    byte = np.maximum(np.where(amax > 0, np.frexp(amax)[1] - 1 + 127, 0) - down, 1)
    scale = np.exp2(byte - 127.0)
    codes = (blocks / scale).astype(np.float32).astype(dtype).astype(np.float64)
    return np.moveaxis((codes * scale).reshape(v.shape), -1, axis)


WIDE = False


def mx_kscale(k):
    if not WIDE:
        return np.ones(k)
    levels = np.array([10, -10, 5, -5, 0])
    if k % 512:
        return np.exp2(np.random.permutation(np.resize(levels, k // 32))).repeat(32)
    a = np.empty((k // 512, 16))
    for p in range(k // 512):
        a[p, :8] = np.random.permutation(np.resize(levels, 8))
        for g in range(8):
            far = levels[np.abs(levels - a[p, g]) >= 10]
            a[p, g + 8] = far[np.random.randint(len(far))]
    return np.exp2(a.ravel()).repeat(32)


def f64(x):
    return np.asarray(x).astype(np.float64)


def striped(idx):
    return np.tile(idx.reshape(-1, 16).T, (8, 1)).astype(np.uint16)


def unstriped(offs):
    return offs[:16].T.reshape(-1).astype(np.int64)


E2M1 = np.array([0.0, 0.5, 1.0, 1.5, 2.0, 3.0, 4.0, 6.0, -0.0, -0.5, -1.0, -1.5, -2.0, -3.0, -4.0, -6.0])


def pack_weight(w, fmt):
    k, n = w.shape
    w = f64(np.asarray(w, np.float32).astype(ml_dtypes.bfloat16)).reshape(k // 32, 32, n)
    amax = np.abs(w).max(1)
    if fmt == "e4m3":
        byte = np.frexp(amax)[1] - 1 + 127 - 7
    else:
        mant, ex = np.frexp(amax / 6.0)
        byte = np.where(mant > 0.5, ex, ex - 1) + 127
    byte = np.clip(np.where(amax > 0, byte, 1), 1, 254)
    scaled = (w * np.exp2(127.0 - byte)[:, None, :]).reshape(k, n).astype(np.float32)
    by_word = np.ascontiguousarray(scaled.reshape(k // 512, 128, 4, n).transpose(0, 1, 3, 2))
    if fmt == "e4m3":
        words = by_word.astype(ml_dtypes.float8_e4m3fn).view(np.uint8)
    else:
        c = by_word.astype(ml_dtypes.float4_e2m1fn).view(np.uint8) & 0xF
        words = (c[..., 0::2] | (c[..., 1::2] << 4)).reshape(k // 512, 128, 2 * n)
    return np.ascontiguousarray(words), np.ascontiguousarray(byte.astype(np.uint8).reshape(k // 512, 16, n))


def unpack_weight(words, scales, fmt):
    g, _, n = scales.shape
    words = np.ascontiguousarray(words).reshape(g, 128, n, -1)
    if fmt == "e4m3":
        vals = words.view(ml_dtypes.float8_e4m3fn).astype(np.float64)
    else:
        nib = np.empty((g, 128, n, 4), np.uint8)
        nib[..., 0::2] = words & 0xF
        nib[..., 1::2] = words >> 4
        vals = E2M1[nib]
    vals = vals * np.repeat(np.exp2(scales.astype(np.float64) - 127.0), 8, axis=1)[..., None]
    return vals.transpose(0, 1, 3, 2).reshape(g * 512, n)


def d_silu(v):
    s = 1.0 / (1.0 + np.exp(-np.maximum(v, -700.0)))
    return s * (1.0 + v * (1.0 - s))


K, T, E, C, H, N = 512, 640, 5, 256, 512, 512


def by_expert(wq, xq):
    return np.concatenate([wq[e].T @ xq[:, e * C:(e + 1) * C] for e in range(E)], axis=1)


def setup_inputs():
    n = np.random.standard_normal
    v = mx_kscale(N)
    u = mx_kscale(H)
    first = np.random.permutation(np.repeat(np.arange(E), T // E))
    second = (first + 1 + np.random.permutation(np.repeat(np.arange(E - 1), -(-T // (E - 1)))[:T])) % E
    while np.bincount(second, minlength=E).max() != T // E:
        load = np.bincount(second, minlength=E); hi, lo = int(load.argmax()), int(load.argmin())
        t = np.flatnonzero((second == hi) & (first != lo))[0]; second[t] = lo
    slot_token = np.empty(E * C, np.int64); pos = np.empty((2, T), np.int64); fill = np.zeros(E, np.int64)
    place = np.stack([np.random.permutation(C) for _ in range(E)])
    for r, deal in enumerate((first, second)):
        for t in np.random.permutation(T):
            e = deal[t]; j = e * C + place[e, fill[e]]; fill[e] += 1; slot_token[j] = t; pos[r, t] = j
    g = np.random.uniform(0.2, 0.8, T)
    w_slot = np.empty(E * C); w_slot[pos[0]] = g; w_slot[pos[1]] = 1.0 - g
    dy = pack_weight(n((N, T)) * v[:, None], "e4m3")
    w2t = pack_weight(n((N, H)) / np.sqrt(N) / v[:, None] * u, "e2m1")
    return {
        "dy_words": dy[0],
        "dy_scales": dy[1],
        "w2t_words": w2t[0],
        "w2t_scales": w2t[1],
        "w1t": (n((E, H, K)) / np.sqrt(H) / u[None, :, None]).astype(np.float32),
        "a": (n((H, E * C))).astype(np.float32),
        "gate": (np.tile(w_slot, (128, 1))).astype(np.float32),
        "offs": striped(slot_token),
        "pos1": striped(pos[0]),
        "pos2": striped(pos[1]),
    }


def reference(dy_words, dy_scales, w2t_words, w2t_scales, w1t, a, gate, offs, pos1, pos2):
    w2t = unpack_weight(w2t_words, w2t_scales, "e2m1")
    w1tq = mxq(f64(w1t), 1, "e4m3")
    idx = unstriped(offs)
    dc = w2t.T @ unpack_weight(dy_words, dy_scales, "e4m3")
    da = f64(gate[:1]) * dc[:, idx] * d_silu(f64(a))
    dx = by_expert(w1tq, mxq(da, 0, "e4m3"))
    out = dx[:, unstriped(pos1)] + dx[:, unstriped(pos2)]
    return out

@@ -1,0 +1,208 @@
+from contextlib import ExitStack
+
+import concourse.mybir as mybir
+from concourse.masks import make_identity
+
+K, T, E, C, H, N = 512, 640, 5, 256, 512, 512
+S = E * C
+P = 128
+FLOPS = 2 * N * H * T + 2 * H * K * S
+
+F32 = mybir.dt.float32
+BF16 = mybir.dt.bfloat16
+I32 = mybir.dt.int32
+U32 = mybir.dt.uint32
+U16 = mybir.dt.uint16
+U8 = mybir.dt.uint8
+FP8X4 = mybir.dt.float8_e4m3fn_x4
+FP4X4 = mybir.dt.float4_e2m1fn_x4
+ALU = mybir.AluOpType
+ACT = mybir.ActivationFunctionType
+
+PIECES = ((0, 512), (512, 1024), (1024, 1280))
+CHUNKS = S // P
+VECTOR_CASTS = ()
+
+
+def tile_moe_sdb_silu_kernel(
+    tc, dy_words, dy_scales, w2t_words, w2t_scales, w1t, a, gate, offs, pos1, pos2, out
+):
+    nc = tc.nc
+    with ExitStack() as ctx:
+        keep = ctx.enter_context(tc.tile_pool(name="keep", bufs=1))
+        ring = ctx.enter_context(tc.tile_pool(name="ring", bufs=3))
+        psum = ctx.enter_context(tc.psum_pool(name="psum", bufs=1))
+        bank = [psum.tile([P, 512], F32, name=f"bank{b}") for b in range(8)]
+
+        planes = keep.tile([P, T + H], U8, align_bytes=64)
+        nc.vector.memset(planes[:].bitcast(I32), 0)
+        warm = keep.tile([P, 8], F32)
+        warm2 = keep.tile([P, 8], F32)
+        nc.vector.memset(warm[:], 0.0)
+        nc.scalar.activation(warm2[:, 0:1], warm[:, 0:1], ACT.Sigmoid)
+
+        dy_sb = keep.tile([P, T], U32, align_bytes=64)
+        nc.sync.dma_start(dy_sb[:].bitcast(I32), dy_words[0].rearrange("p t d -> p (t d)").bitcast(I32))
+        w2_sb = keep.tile([P, 2 * H], U8, align_bytes=64)
+        nc.sync.dma_start(w2_sb[:].bitcast(I32), w2t_words[0].bitcast(I32))
+        a_sb = [keep.tile([P, S], F32, name=f"a{c}") for c in range(4)]
+        nc.sync.dma_start(a_sb[0][:], a[0:P, :])
+        for r in range(4):
+            nc.sync.dma_start(planes[r:P:32, 0:T].bitcast(I32), dy_scales[0, r:16:4, :].bitcast(I32))
+            nc.sync.dma_start(planes[r:P:32, T : T + H].bitcast(I32), w2t_scales[0, r:16:4, :].bitcast(I32))
+        offs_sb = keep.tile([P, S // 16], U16)
+        nc.sync.dma_start(offs_sb[:], offs)
+        for c in range(1, 4):
+            nc.sync.dma_start(a_sb[c][:], a[c * P : (c + 1) * P, :])
+        gate_rows = keep.tile([P, P], F32)
+        nc.gpsimd.memset(gate_rows[:], 0.0)
+        ident = keep.tile([P, P], F32)
+        make_identity(nc, ident[:])
+        nc.sync.dma_start(gate_rows[0:CHUNKS, :], gate[0].rearrange("(c p) -> c p", p=P))
+        w1_raw = [keep.tile([P, 4, K], F32, name=f"w1raw{e}") for e in range(E)]
+        for e in range(E):
+            nc.sync.dma_start(w1_raw[e][:], w1t[e].rearrange("(p j) k -> p j k", j=4))
+        pos1_sb = keep.tile([P, T // 16], U16)
+        nc.sync.dma_start(pos1_sb[:], pos1)
+        pos2_sb = keep.tile([P, T // 16], U16)
+        nc.sync.dma_start(pos2_sb[:], pos2)
+
+        dc = [keep.tile([P, T], F32, name=f"dc{c}") for c in range(4)]
+        sg = [keep.tile([P, S], F32, name=f"sg{c}") for c in range(4)]
+        ga = [keep.tile([P, S], F32, name=f"ga{c}") for c in range(4)]
+        for c in range(4):
+            for b, lo, hi in ((c, 0, 512), (4 + c, 512, T)):
+                nc.tensor.matmul_mx(
+                    out=bank[b][:, 0 : hi - lo],
+                    lhsT=w2_sb[:, 2 * P * c : 2 * P * (c + 1)].bitcast(FP4X4),
+                    lhsT_scale=planes[:, T + P * c : T + P * (c + 1)],
+                    rhs=dy_sb[:, lo:hi].bitcast(FP8X4),
+                    rhs_scale=planes[:, lo:hi],
+                    start=True,
+                    stop=True,
+                )
+        for c in range(4):
+            if c == 0:
+                for lo, hi in PIECES:
+                    nc.scalar.activation(sg[c][:, lo:hi], a_sb[c][:, lo:hi], ACT.Sigmoid)
+                nc.vector.tensor_copy(dc[c][:, 0:512], bank[c][:])
+                nc.vector.tensor_copy(dc[c][:, 512:T], bank[4 + c][:, 0 : T - 512])
+            else:
+                nc.scalar.copy(dc[c][:, 0:512], bank[c][:])
+                nc.scalar.copy(dc[c][:, 512:T], bank[4 + c][:, 0 : T - 512])
+                nc.scalar.activation(sg[c][:], a_sb[c][:], ACT.Sigmoid)
+            for lo, hi in PIECES:
+                nc.vector.tensor_tensor(
+                    ga[c][:, lo:hi], dc[c][:].indirect(offs_sb[:, lo // 16 : hi // 16]), sg[c][:, lo:hi], ALU.mult
+                )
+
+        nc.tensor.transpose(bank[7][:, P : 2 * P], gate_rows[:], ident[:])
+        neg_gate = keep.tile([P, 16], F32)
+        nc.vector.tensor_scalar(neg_gate[:, 0:CHUNKS], bank[7][:, P : P + CHUNKS], -1.0, None, ALU.mult)
+
+        def turn(src, j, b):
+            for c in range(4):
+                nc.tensor.transpose(bank[b][:, c * P : (c + 1) * P], src[c][:, j * P : (j + 1) * P], ident[:])
+
+        def paired(b):
+            return bank[b][:].rearrange("s (p u e) -> s u p e", u=2, e=2)
+
+        yt = [keep.tile([P, H], F32, name=f"yt{j}") for j in range(CHUNKS)]
+        for j in range(CHUNKS):
+            turn(a_sb, j, j % 4)
+            nc.scalar.activation(
+                yt[j][:].rearrange("s (u p e) -> s u p e", u=2, e=2), paired(j % 4), ACT.Silu, scale=-1.0
+            )
+
+        w1_codes = {}
+        w1_scales = {}
+
+        def cast_w1(e, h):
+            grouped = ring.tile([P, 256, 4], BF16, name="w1grouped", align_bytes=64)
+            dst = grouped[:].rearrange("p (c i) t -> p c t i", i=4)
+            src = w1_raw[e][:, :, 256 * h : 256 * (h + 1)].rearrange("p t (c i) -> p c t i", i=4)
+            if (e, h) in VECTOR_CASTS:
+                nc.vector.tensor_copy(dst, src)
+            else:
+                nc.scalar.copy(dst, src)
+            return grouped
+
+        def quantize_w1(e, h, grouped):
+            w1_codes[e, h] = keep.tile([P, 256], U32, name=f"w1codes{e}_{h}", align_bytes=64)
+            w1_scales[e, h] = keep.tile([P, 256], U8, name=f"w1scales{e}_{h}", align_bytes=64)
+            nc.vector.quantize_mx(
+                out=w1_codes[e, h][:].bitcast(FP8X4),
+                scales=w1_scales[e, h][:],
+                in_=grouped[:].rearrange("p k t -> p (k t)"),
+            )
+
+        def factor(j):
+            nc.vector.tensor_scalar(yt[j][:], yt[j][:], 1.0, neg_gate[:, j : j + 1], ALU.subtract, ALU.mult)
+
+        da_codes = [keep.tile([P, C], U32, name=f"dacodes{e}", align_bytes=64) for e in range(E)]
+        da_scales = [keep.tile([P, C], U8, name=f"dascales{e}", align_bytes=64) for e in range(E)]
+        da_bf = [keep.tile([P, 4 * C], BF16, name=f"dabf{e}", align_bytes=64) for e in range(E)]
+
+        def quantize_da(e):
+            nc.vector.quantize_mx(out=da_codes[e][:].bitcast(FP8X4), scales=da_scales[e][:], in_=da_bf[e][:])
+
+        factor(0)
+        factor(1)
+        for e in range(E):
+            back = bank[4 + e % 2]
+            grouped = cast_w1(e, 0)
+            for jj in range(2):
+                j = 2 * e + jj
+                b = (CHUNKS + j) % 4
+                turn(ga, j, b)
+                dat = ring.tile([P, H], BF16, name="dat")
+                nc.vector.tensor_tensor(
+                    dat[:].rearrange("s (u p e) -> s u p e", u=2, e=2),
+                    paired(b),
+                    yt[j][:].rearrange("s (u p e) -> s u p e", u=2, e=2),
+                    ALU.mult,
+                )
+                if j + 2 < CHUNKS:
+                    factor(j + 2)
+                words = dat[:].bitcast(F32)
+                for u in range(2):
+                    q = 2 * jj + u
+                    nc.tensor.transpose(back[:, q * P : (q + 1) * P], words[:, u * P : (u + 1) * P], ident[:])
+            nc.scalar.copy(
+                da_bf[e][:].bitcast(F32).rearrange("p (j s u) -> p j s u", j=2, u=2),
+                back[:].rearrange("p (j u s) -> p j s u", j=2, u=2),
+            )
+            quantize_w1(e, 0, grouped)
+            if e > 0:
+                quantize_da(e - 1)
+        quantize_da(E - 1)
+
+        dx_banks = (6, 7, 0, 1, 2, 3, 4, 5, 6, 7, 0, 1)
+        for kb in range(4):
+            h, k0 = kb // 2, (kb % 2) * P
+            dx = keep.tile([P, S], F32, name=f"dx{kb}")
+            for g, (lo, hi) in enumerate(PIECES):
+                b = dx_banks[3 * kb + g]
+                for e in range(lo // C, hi // C):
+                    nc.tensor.matmul_mx(
+                        out=bank[b][:, e * C - lo : (e + 1) * C - lo],
+                        lhsT=w1_codes[e, h][:, k0 : k0 + P].bitcast(FP8X4),
+                        lhsT_scale=w1_scales[e, h][:, k0 : k0 + P],
+                        rhs=da_codes[e][:].bitcast(FP8X4),
+                        rhs_scale=da_scales[e][:],
+                        start=True,
+                        stop=True,
+                    )
+                nc.scalar.copy(dx[:, lo:hi], bank[b][:, 0 : hi - lo])
+            first = ring.tile([P, T], F32, name="first")
+            nc.vector.tensor_copy(first[:], dx[:].indirect(pos1_sb[:]))
+            if kb == 0:
+                for e in range(E):
+                    quantize_w1(e, 1, cast_w1(e, 1))
+            both = ring.tile([P, T], F32, name="both")
+            cuts = ((0, T),) if kb < 3 else ((0, 416), (416, T))
+            for lo, hi in cuts:
+                nc.vector.tensor_tensor(
+                    both[:, lo:hi], dx[:].indirect(pos2_sb[:, lo // 16 : hi // 16]), first[:, lo:hi], ALU.add
+                )
+                nc.sync.dma_start(out[kb * P : (kb + 1) * P, lo:hi], both[:, lo:hi])

@@ -21,7 +21,11 @@ ACT = mybir.ActivationFunctionType
 
 PIECES = ((0, 512), (512, 1024), (1024, 1280))
 CHUNKS = S // P
-VECTOR_CASTS = ()
+VECTOR_CASTS = ((1, 2), (2, 2), (3, 2), (3, 1))
+WINDOW = S + 32
+FIRST = ((0, 512), (512, S))
+GROUPS = ((0, 4), (4, 5))
+PAIRS = ((0, 2), (2, 4), (4, 5))
 
 
 def tile_moe_sdb_silu_kernel(
@@ -31,11 +35,12 @@ def tile_moe_sdb_silu_kernel(
     with ExitStack() as ctx:
         keep = ctx.enter_context(tc.tile_pool(name="keep", bufs=1))
         ring = ctx.enter_context(tc.tile_pool(name="ring", bufs=3))
+        rows = ctx.enter_context(tc.tile_pool(name="rows", bufs=4))
         psum = ctx.enter_context(tc.psum_pool(name="psum", bufs=1))
         bank = [psum.tile([P, 512], F32, name=f"bank{b}") for b in range(8)]
 
         planes = keep.tile([P, T + H], U8, align_bytes=64)
-        nc.vector.memset(planes[:].bitcast(I32), 0)
+        nc.gpsimd.memset(planes[:].bitcast(I32), 0)
         warm = keep.tile([P, 8], F32)
         warm2 = keep.tile([P, 8], F32)
         nc.vector.memset(warm[:], 0.0)
@@ -45,13 +50,18 @@ def tile_moe_sdb_silu_kernel(
         nc.sync.dma_start(dy_sb[:].bitcast(I32), dy_words[0].rearrange("p t d -> p (t d)").bitcast(I32))
         w2_sb = keep.tile([P, 2 * H], U8, align_bytes=64)
         nc.sync.dma_start(w2_sb[:].bitcast(I32), w2t_words[0].bitcast(I32))
-        a_sb = [keep.tile([P, S], F32, name=f"a{c}") for c in range(4)]
-        nc.sync.dma_start(a_sb[0][:], a[0:P, :])
+        a_sb = [rows.tile([P, S], F32, name=f"a{c}", tag="rows") for c in range(4)]
+        offs_sb = keep.tile([P, S // 16], U16)
+        nc.sync.dma_start(offs_sb[:], offs)
+        pos1_sb = keep.tile([P, T // 16], U16)
+        nc.sync.dma_start(pos1_sb[:], pos1)
+        pos2_sb = keep.tile([P, T // 16], U16)
+        nc.sync.dma_start(pos2_sb[:], pos2)
         for r in range(4):
             nc.sync.dma_start(planes[r:P:32, 0:T].bitcast(I32), dy_scales[0, r:16:4, :].bitcast(I32))
             nc.sync.dma_start(planes[r:P:32, T : T + H].bitcast(I32), w2t_scales[0, r:16:4, :].bitcast(I32))
-        offs_sb = keep.tile([P, S // 16], U16)
-        nc.sync.dma_start(offs_sb[:], offs)
+        nc.sync.dma_start(a_sb[0][:, 0:512], a[0:P, 0:512])
+        nc.sync.dma_start(a_sb[0][:, 512:S], a[0:P, 512:S])
         for c in range(1, 4):
             nc.sync.dma_start(a_sb[c][:], a[c * P : (c + 1) * P, :])
         gate_rows = keep.tile([P, P], F32)
@@ -59,15 +69,13 @@ def tile_moe_sdb_silu_kernel(
         ident = keep.tile([P, P], F32)
         make_identity(nc, ident[:])
         nc.sync.dma_start(gate_rows[0:CHUNKS, :], gate[0].rearrange("(c p) -> c p", p=P))
-        w1_raw = [keep.tile([P, 4, K], F32, name=f"w1raw{e}") for e in range(E)]
-        for e in range(E):
-            nc.sync.dma_start(w1_raw[e][:], w1t[e].rearrange("(p j) k -> p j k", j=4))
-        pos1_sb = keep.tile([P, T // 16], U16)
-        nc.sync.dma_start(pos1_sb[:], pos1)
-        pos2_sb = keep.tile([P, T // 16], U16)
-        nc.sync.dma_start(pos2_sb[:], pos2)
+        w1_raw = [keep.tile([P, hi - lo, 4, K], F32, name=f"w1raw{lo}") for lo, hi in PAIRS]
+        for g, (lo, hi) in enumerate(PAIRS):
+            nc.sync.dma_start(w1_raw[g][:], w1t[lo:hi].rearrange("e (p j) k -> p e j k", j=4))
 
-        dc = [keep.tile([P, T], F32, name=f"dc{c}") for c in range(4)]
+        dc = [keep.tile([P, WINDOW], F32, name=f"dc{c}") for c in range(4)]
+        for c in range(4):
+            nc.vector.memset(dc[c][:, T:WINDOW], 0.0)
         sg = [keep.tile([P, S], F32, name=f"sg{c}") for c in range(4)]
         ga = [keep.tile([P, S], F32, name=f"ga{c}") for c in range(4)]
         for c in range(4):
@@ -83,7 +91,7 @@ def tile_moe_sdb_silu_kernel(
                 )
         for c in range(4):
             if c == 0:
-                for lo, hi in PIECES:
+                for lo, hi in FIRST:
                     nc.scalar.activation(sg[c][:, lo:hi], a_sb[c][:, lo:hi], ACT.Sigmoid)
                 nc.vector.tensor_copy(dc[c][:, 0:512], bank[c][:])
                 nc.vector.tensor_copy(dc[c][:, 512:T], bank[4 + c][:, 0 : T - 512])
@@ -91,7 +99,7 @@ def tile_moe_sdb_silu_kernel(
                 nc.scalar.copy(dc[c][:, 0:512], bank[c][:])
                 nc.scalar.copy(dc[c][:, 512:T], bank[4 + c][:, 0 : T - 512])
                 nc.scalar.activation(sg[c][:], a_sb[c][:], ACT.Sigmoid)
-            for lo, hi in PIECES:
+            for lo, hi in FIRST if c in (0, 3) else ((0, S),):
                 nc.vector.tensor_tensor(
                     ga[c][:, lo:hi], dc[c][:].indirect(offs_sb[:, lo // 16 : hi // 16]), sg[c][:, lo:hi], ALU.mult
                 )
@@ -109,100 +117,139 @@ def tile_moe_sdb_silu_kernel(
 
         yt = [keep.tile([P, H], F32, name=f"yt{j}") for j in range(CHUNKS)]
         for j in range(CHUNKS):
-            turn(a_sb, j, j % 4)
+            turn(a_sb, j, j % 8)
             nc.scalar.activation(
-                yt[j][:].rearrange("s (u p e) -> s u p e", u=2, e=2), paired(j % 4), ACT.Silu, scale=-1.0
+                yt[j][:].rearrange("s (u p e) -> s u p e", u=2, e=2), paired(j % 8), ACT.Silu, scale=-1.0
             )
 
-        w1_codes = {}
-        w1_scales = {}
+        w1_bf = [keep.tile([P, E * 512], BF16, name=f"w1bf{kb}", align_bytes=64) for kb in range(4)]
+        w1_codes = [keep.tile([P, E * P], U32, name=f"w1codes{kb}", align_bytes=64) for kb in range(4)]
+        w1_scales = [keep.tile([P, E * P], U8, name=f"w1scales{kb}", align_bytes=64) for kb in range(4)]
 
-        def cast_w1(e, h):
-            grouped = ring.tile([P, 256, 4], BF16, name="w1grouped", align_bytes=64)
-            dst = grouped[:].rearrange("p (c i) t -> p c t i", i=4)
-            src = w1_raw[e][:, :, 256 * h : 256 * (h + 1)].rearrange("p t (c i) -> p c t i", i=4)
-            if (e, h) in VECTOR_CASTS:
+        def cast_w1(kb, g):
+            lo, hi = PAIRS[g]
+            dst = w1_bf[kb][:, lo * 512 : hi * 512].rearrange("p (e c i t) -> p e c t i", e=hi - lo, i=4, t=4)
+            src = w1_raw[g][:, :, :, P * kb : P * (kb + 1)].rearrange("p e t (c i) -> p e c t i", i=4)
+            if (kb, g) in VECTOR_CASTS:
                 nc.vector.tensor_copy(dst, src)
             else:
                 nc.scalar.copy(dst, src)
-            return grouped
 
-        def quantize_w1(e, h, grouped):
-            w1_codes[e, h] = keep.tile([P, 256], U32, name=f"w1codes{e}_{h}", align_bytes=64)
-            w1_scales[e, h] = keep.tile([P, 256], U8, name=f"w1scales{e}_{h}", align_bytes=64)
+        def quantize_w1(kb, lo, hi):
             nc.vector.quantize_mx(
-                out=w1_codes[e, h][:].bitcast(FP8X4),
-                scales=w1_scales[e, h][:],
-                in_=grouped[:].rearrange("p k t -> p (k t)"),
+                out=w1_codes[kb][:, lo * P : hi * P].bitcast(FP8X4),
+                scales=w1_scales[kb][:, lo * P : hi * P],
+                in_=w1_bf[kb][:, lo * 512 : hi * 512],
             )
 
         def factor(j):
             nc.vector.tensor_scalar(yt[j][:], yt[j][:], 1.0, neg_gate[:, j : j + 1], ALU.subtract, ALU.mult)
 
-        da_codes = [keep.tile([P, C], U32, name=f"dacodes{e}", align_bytes=64) for e in range(E)]
-        da_scales = [keep.tile([P, C], U8, name=f"dascales{e}", align_bytes=64) for e in range(E)]
-        da_bf = [keep.tile([P, 4 * C], BF16, name=f"dabf{e}", align_bytes=64) for e in range(E)]
+        da_codes = {lo: keep.tile([P, (hi - lo) * C], U32, name=f"dacodes{lo}", align_bytes=64) for lo, hi in PAIRS}
+        da_scales = {lo: keep.tile([P, (hi - lo) * C], U8, name=f"dascales{lo}", align_bytes=64) for lo, hi in PAIRS}
+        da_bf = {lo: keep.tile([P, (hi - lo) * 4 * C], BF16, name=f"dabf{lo}", align_bytes=64) for lo, hi in PAIRS}
 
-        def quantize_da(e):
-            nc.vector.quantize_mx(out=da_codes[e][:].bitcast(FP8X4), scales=da_scales[e][:], in_=da_bf[e][:])
+        def quantize_da(lo):
+            nc.vector.quantize_mx(out=da_codes[lo][:].bitcast(FP8X4), scales=da_scales[lo][:], in_=da_bf[lo][:])
 
-        factor(0)
-        factor(1)
-        for e in range(E):
-            back = bank[4 + e % 2]
-            grouped = cast_w1(e, 0)
-            for jj in range(2):
-                j = 2 * e + jj
-                b = (CHUNKS + j) % 4
-                turn(ga, j, b)
-                dat = ring.tile([P, H], BF16, name="dat")
-                nc.vector.tensor_tensor(
-                    dat[:].rearrange("s (u p e) -> s u p e", u=2, e=2),
-                    paired(b),
-                    yt[j][:].rearrange("s (u p e) -> s u p e", u=2, e=2),
-                    ALU.mult,
-                )
-                if j + 2 < CHUNKS:
-                    factor(j + 2)
-                words = dat[:].bitcast(F32)
-                for u in range(2):
-                    q = 2 * jj + u
-                    nc.tensor.transpose(back[:, q * P : (q + 1) * P], words[:, u * P : (u + 1) * P], ident[:])
-            nc.scalar.copy(
-                da_bf[e][:].bitcast(F32).rearrange("p (j s u) -> p j s u", j=2, u=2),
-                back[:].rearrange("p (j u s) -> p j s u", j=2, u=2),
+        def finish(j):
+            b = 2 + j % 4
+            back = bank[6 + (j // 2) % 2]
+            turn(ga, j, b)
+            dat = keep.tile([P, H], BF16, name=f"dat{j}")
+            nc.vector.tensor_tensor(
+                dat[:].rearrange("s (u p e) -> s u p e", u=2, e=2),
+                paired(b),
+                yt[j][:].rearrange("s (u p e) -> s u p e", u=2, e=2),
+                ALU.mult,
             )
-            quantize_w1(e, 0, grouped)
-            if e > 0:
-                quantize_da(e - 1)
-        quantize_da(E - 1)
+            words = dat[:].bitcast(F32)
+            for u in range(2):
+                q = 2 * (j % 2) + u
+                nc.tensor.transpose(back[:, q * P : (q + 1) * P], words[:, u * P : (u + 1) * P], ident[:])
 
-        dx_banks = (6, 7, 0, 1, 2, 3, 4, 5, 6, 7, 0, 1)
-        for kb in range(4):
-            h, k0 = kb // 2, (kb % 2) * P
-            dx = keep.tile([P, S], F32, name=f"dx{kb}")
-            for g, (lo, hi) in enumerate(PIECES):
-                b = dx_banks[3 * kb + g]
-                for e in range(lo // C, hi // C):
-                    nc.tensor.matmul_mx(
-                        out=bank[b][:, e * C - lo : (e + 1) * C - lo],
-                        lhsT=w1_codes[e, h][:, k0 : k0 + P].bitcast(FP8X4),
-                        lhsT_scale=w1_scales[e, h][:, k0 : k0 + P],
-                        rhs=da_codes[e][:].bitcast(FP8X4),
-                        rhs_scale=da_scales[e][:],
-                        start=True,
-                        stop=True,
-                    )
-                nc.scalar.copy(dx[:, lo:hi], bank[b][:, 0 : hi - lo])
-            first = ring.tile([P, T], F32, name="first")
-            nc.vector.tensor_copy(first[:], dx[:].indirect(pos1_sb[:]))
-            if kb == 0:
-                for e in range(E):
-                    quantize_w1(e, 1, cast_w1(e, 1))
-            both = ring.tile([P, T], F32, name="both")
+        def unturn(e, lo=0, hi=2):
+            dst = da_bf[e - e % 2][:, (e % 2) * 4 * C : (e % 2 + 1) * 4 * C].bitcast(F32)
+            nc.scalar.copy(
+                dst.rearrange("p (j s u) -> p j s u", j=2, u=2)[:, lo:hi],
+                bank[6 + e % 2][:].rearrange("p (j u s) -> p j s u", j=2, u=2)[:, lo:hi],
+            )
+
+        dx_banks = (0, 1, 2, 3, 4, 5, 6, 7, 0, 1, 2, 3)
+        dx = [rows.tile([P, S], F32, name=f"dx{kb}", tag="rows") for kb in range(4)]
+
+        def product(kb, g):
+            lo, hi = PIECES[g]
+            b = dx_banks[3 * kb + g]
+            for e in range(lo // C, hi // C):
+                d0, dk = e - e % 2, (e % 2) * C
+                nc.tensor.matmul_mx(
+                    out=bank[b][:, e * C - lo : (e + 1) * C - lo],
+                    lhsT=w1_codes[kb][:, e * P : (e + 1) * P].bitcast(FP8X4),
+                    lhsT_scale=w1_scales[kb][:, e * P : (e + 1) * P],
+                    rhs=da_codes[d0][:, dk : dk + C].bitcast(FP8X4),
+                    rhs_scale=da_scales[d0][:, dk : dk + C],
+                    start=True,
+                    stop=True,
+                )
+            nc.scalar.copy(dx[kb][:, lo:hi], bank[b][:, 0 : hi - lo])
+
+        first = {}
+
+        def fetch(kb):
+            first[kb] = ring.tile([P, T], F32, name="first")
+            nc.vector.tensor_copy(first[kb][:], dx[kb][:].indirect(pos1_sb[:]))
+
+        def combine(kb):
+            if kb in (1, 2):
+                both = w1_bf[kb + 1][:, E * 512 - 2 * T :].bitcast(F32)
+            else:
+                both = ring.tile([P, T], F32, name="both")
             cuts = ((0, T),) if kb < 3 else ((0, 416), (416, T))
             for lo, hi in cuts:
                 nc.vector.tensor_tensor(
-                    both[:, lo:hi], dx[:].indirect(pos2_sb[:, lo // 16 : hi // 16]), first[:, lo:hi], ALU.add
+                    both[:, lo:hi], dx[kb][:].indirect(pos2_sb[:, lo // 16 : hi // 16]), first[kb][:, lo:hi], ALU.add
                 )
                 nc.sync.dma_start(out[kb * P : (kb + 1) * P, lo:hi], both[:, lo:hi])
+
+        for j in range(2):
+            factor(j)
+        for j in range(CHUNKS):
+            finish(j)
+            if j + 2 < CHUNKS:
+                factor(j + 2)
+            if j % 2 == 1 and j < 8:
+                e = j // 2
+                cast_w1(e // 3, e % 3)
+                unturn(e)
+            if j >= 8:
+                unturn(4, j - 8, j - 7)
+        quantize_da(0)
+        for lo, hi in GROUPS:
+            quantize_w1(0, lo, hi)
+        quantize_da(2)
+        quantize_da(4)
+        cast_w1(1, 1)
+        for g in range(3):
+            product(0, g)
+        cast_w1(1, 2)
+        for lo, hi in GROUPS:
+            quantize_w1(1, lo, hi)
+        cast_w1(2, 2)
+        fetch(0)
+        cast_w1(2, 0)
+        for g in range(3):
+            product(1, g)
+        cast_w1(2, 1)
+        combine(0)
+        for kb in (2, 3):
+            if kb == 3:
+                for g in range(3):
+                    cast_w1(3, g)
+            fetch(kb - 1)
+            for g in (0, 2, 1):
+                quantize_w1(kb, *PAIRS[g])
+                product(kb, g)
+            combine(kb - 1)
+        fetch(3)
+        combine(3)

@@ -21,7 +21,10 @@ ACT = mybir.ActivationFunctionType
 
 PIECES = ((0, 512), (512, 1024), (1024, 1280))
 CHUNKS = S // P
-VECTOR_CASTS = ((1, 2), (2, 2), (3, 2), (3, 1))
+VECTOR_CASTS = ((1, 1),)
+AFTER_LAST = ((1, 1),)
+GATE_AT = 3
+HALVES = ((0, 384), (384, T))
 WINDOW = S + 32
 FIRST = ((0, 512), (512, S))
 GROUPS = ((0, 4), (4, 5))
@@ -51,16 +54,18 @@ def tile_moe_sdb_silu_kernel(
         w2_sb = keep.tile([P, 2 * H], U8, align_bytes=64)
         nc.sync.dma_start(w2_sb[:].bitcast(I32), w2t_words[0].bitcast(I32))
         a_sb = [rows.tile([P, S], F32, name=f"a{c}", tag="rows") for c in range(4)]
-        offs_sb = keep.tile([P, S // 16], U16)
-        nc.sync.dma_start(offs_sb[:], offs)
-        pos1_sb = keep.tile([P, T // 16], U16)
-        nc.sync.dma_start(pos1_sb[:], pos1)
-        pos2_sb = keep.tile([P, T // 16], U16)
-        nc.sync.dma_start(pos2_sb[:], pos2)
+        w1_last = [keep.tile([P, 4, 256], F32, name=f"w1last{h}") for h in range(2)]
         for r in range(4):
             nc.sync.dma_start(planes[r:P:32, 0:T].bitcast(I32), dy_scales[0, r:16:4, :].bitcast(I32))
             nc.sync.dma_start(planes[r:P:32, T : T + H].bitcast(I32), w2t_scales[0, r:16:4, :].bitcast(I32))
+            if r == 1:
+                for h in range(2):
+                    nc.sync.dma_start(
+                        w1_last[h][:], w1t[E - 1, :, 256 * h : 256 * (h + 1)].rearrange("(p j) k -> p j k", j=4)
+                    )
         nc.sync.dma_start(a_sb[0][:, 0:512], a[0:P, 0:512])
+        offs_sb = keep.tile([P, S // 16], U16)
+        nc.sync.dma_start(offs_sb[:], offs)
         nc.sync.dma_start(a_sb[0][:, 512:S], a[0:P, 512:S])
         for c in range(1, 4):
             nc.sync.dma_start(a_sb[c][:], a[c * P : (c + 1) * P, :])
@@ -69,9 +74,13 @@ def tile_moe_sdb_silu_kernel(
         ident = keep.tile([P, P], F32)
         make_identity(nc, ident[:])
         nc.sync.dma_start(gate_rows[0:CHUNKS, :], gate[0].rearrange("(c p) -> c p", p=P))
-        w1_raw = [keep.tile([P, hi - lo, 4, K], F32, name=f"w1raw{lo}") for lo, hi in PAIRS]
-        for g, (lo, hi) in enumerate(PAIRS):
+        w1_raw = [keep.tile([P, hi - lo, 4, K], F32, name=f"w1raw{lo}") for lo, hi in PAIRS[:2]]
+        for g, (lo, hi) in enumerate(PAIRS[:2]):
             nc.sync.dma_start(w1_raw[g][:], w1t[lo:hi].rearrange("e (p j) k -> p e j k", j=4))
+        pos1_sb = keep.tile([P, T // 16], U16)
+        nc.sync.dma_start(pos1_sb[:], pos1)
+        pos2_sb = keep.tile([P, T // 16], U16)
+        nc.sync.dma_start(pos2_sb[:], pos2)
 
         dc = [keep.tile([P, WINDOW], F32, name=f"dc{c}") for c in range(4)]
         for c in range(4):
@@ -79,9 +88,10 @@ def tile_moe_sdb_silu_kernel(
         sg = [keep.tile([P, S], F32, name=f"sg{c}") for c in range(4)]
         ga = [keep.tile([P, S], F32, name=f"ga{c}") for c in range(4)]
         for c in range(4):
-            for b, lo, hi in ((c, 0, 512), (4 + c, 512, T)):
+            cuts = ((c, 0, 0, 512), (4 + c, 0, 512, T)) if c else ((0, 0, 0, 256), (4, 0, 256, 512), (4, 256, 512, T))
+            for b, at, lo, hi in cuts:
                 nc.tensor.matmul_mx(
-                    out=bank[b][:, 0 : hi - lo],
+                    out=bank[b][:, at : at + hi - lo],
                     lhsT=w2_sb[:, 2 * P * c : 2 * P * (c + 1)].bitcast(FP4X4),
                     lhsT_scale=planes[:, T + P * c : T + P * (c + 1)],
                     rhs=dy_sb[:, lo:hi].bitcast(FP8X4),
@@ -93,20 +103,32 @@ def tile_moe_sdb_silu_kernel(
             if c == 0:
                 for lo, hi in FIRST:
                     nc.scalar.activation(sg[c][:, lo:hi], a_sb[c][:, lo:hi], ACT.Sigmoid)
-                nc.vector.tensor_copy(dc[c][:, 0:512], bank[c][:])
-                nc.vector.tensor_copy(dc[c][:, 512:T], bank[4 + c][:, 0 : T - 512])
+                nc.vector.tensor_copy(dc[c][:, 0:256], bank[c][:, 0:256])
+                nc.vector.tensor_copy(dc[c][:, 256:T], bank[4 + c][:, 0 : T - 256])
             else:
                 nc.scalar.copy(dc[c][:, 0:512], bank[c][:])
                 nc.scalar.copy(dc[c][:, 512:T], bank[4 + c][:, 0 : T - 512])
                 nc.scalar.activation(sg[c][:], a_sb[c][:], ACT.Sigmoid)
-            for lo, hi in FIRST if c in (0, 3) else ((0, S),):
+            for lo, hi in (FIRST, ((0, S),), ((0, S),), ((0, 768), (768, S)))[c]:
                 nc.vector.tensor_tensor(
                     ga[c][:, lo:hi], dc[c][:].indirect(offs_sb[:, lo // 16 : hi // 16]), sg[c][:, lo:hi], ALU.mult
                 )
 
-        nc.tensor.transpose(bank[7][:, P : 2 * P], gate_rows[:], ident[:])
+        last_codes = keep.tile([P, K], U32, align_bytes=64)
+        last_scales = keep.tile([P, K], U8, align_bytes=64)
+        for h in range(2):
+            last_bf = keep.tile([P, 1024], BF16, name=f"lastbf{h}", align_bytes=64)
+            nc.vector.tensor_copy(
+                last_bf[:].rearrange("p (c i t) -> p c t i", i=4, t=4),
+                w1_last[h][:].rearrange("p t (c i) -> p c t i", i=4),
+            )
+            nc.vector.quantize_mx(
+                out=last_codes[:, 256 * h : 256 * (h + 1)].bitcast(FP8X4),
+                scales=last_scales[:, 256 * h : 256 * (h + 1)],
+                in_=last_bf[:],
+            )
+
         neg_gate = keep.tile([P, 16], F32)
-        nc.vector.tensor_scalar(neg_gate[:, 0:CHUNKS], bank[7][:, P : P + CHUNKS], -1.0, None, ALU.mult)
 
         def turn(src, j, b):
             for c in range(4):
@@ -121,14 +143,24 @@ def tile_moe_sdb_silu_kernel(
             nc.scalar.activation(
                 yt[j][:].rearrange("s (u p e) -> s u p e", u=2, e=2), paired(j % 8), ACT.Silu, scale=-1.0
             )
+            if j == GATE_AT:
+                nc.tensor.transpose(bank[j][:, 0:P], gate_rows[:], ident[:])
+                nc.scalar.activation(neg_gate[:, 0:CHUNKS], bank[j][:, 0:CHUNKS], ACT.Copy, scale=-1.0)
 
-        w1_bf = [keep.tile([P, E * 512], BF16, name=f"w1bf{kb}", align_bytes=64) for kb in range(4)]
-        w1_codes = [keep.tile([P, E * P], U32, name=f"w1codes{kb}", align_bytes=64) for kb in range(4)]
-        w1_scales = [keep.tile([P, E * P], U8, name=f"w1scales{kb}", align_bytes=64) for kb in range(4)]
+        w1_bf = [keep.tile([P, 2048 if kb == 0 else 1024], BF16, name=f"w1bf{kb}", align_bytes=64) for kb in range(3)]
+        w1_codes = [keep.tile([P, 4 * P], U32, name=f"w1codes{kb}", align_bytes=64) for kb in range(4)]
+        w1_scales = [keep.tile([P, 4 * P], U8, name=f"w1scales{kb}", align_bytes=64) for kb in range(4)]
+
+        def staged(kb, g):
+            if kb == 3:
+                return first[g][:].bitcast(BF16)[:, 0:1024]
+            if kb > 0 and g == 1:
+                return da_bf[4][:, 0:1024]
+            return w1_bf[kb][:, g * 1024 : (g + 1) * 1024]
 
         def cast_w1(kb, g):
             lo, hi = PAIRS[g]
-            dst = w1_bf[kb][:, lo * 512 : hi * 512].rearrange("p (e c i t) -> p e c t i", e=hi - lo, i=4, t=4)
+            dst = staged(kb, g).rearrange("p (e c i t) -> p e c t i", e=hi - lo, i=4, t=4)
             src = w1_raw[g][:, :, :, P * kb : P * (kb + 1)].rearrange("p e t (c i) -> p e c t i", i=4)
             if (kb, g) in VECTOR_CASTS:
                 nc.vector.tensor_copy(dst, src)
@@ -139,7 +171,7 @@ def tile_moe_sdb_silu_kernel(
             nc.vector.quantize_mx(
                 out=w1_codes[kb][:, lo * P : hi * P].bitcast(FP8X4),
                 scales=w1_scales[kb][:, lo * P : hi * P],
-                in_=w1_bf[kb][:, lo * 512 : hi * 512],
+                in_=staged(kb, lo // 2) if hi - lo == 2 else w1_bf[kb][:],
             )
 
         def factor(j):
@@ -147,14 +179,17 @@ def tile_moe_sdb_silu_kernel(
 
         da_codes = {lo: keep.tile([P, (hi - lo) * C], U32, name=f"dacodes{lo}", align_bytes=64) for lo, hi in PAIRS}
         da_scales = {lo: keep.tile([P, (hi - lo) * C], U8, name=f"dascales{lo}", align_bytes=64) for lo, hi in PAIRS}
-        da_bf = {lo: keep.tile([P, (hi - lo) * 4 * C], BF16, name=f"dabf{lo}", align_bytes=64) for lo, hi in PAIRS}
+        da_bf = {lo: keep.tile([P, max((hi - lo) * 4 * C, 2 * T)], BF16, name=f"dabf{lo}", align_bytes=64) for lo, hi in PAIRS}
 
         def quantize_da(lo):
-            nc.vector.quantize_mx(out=da_codes[lo][:].bitcast(FP8X4), scales=da_scales[lo][:], in_=da_bf[lo][:])
+            nc.vector.quantize_mx(out=da_codes[lo][:].bitcast(FP8X4), scales=da_scales[lo][:], in_=da_bf[lo][:, 0 : 1024 if lo == 4 else 2048])
+
+        def back_bank(j):
+            return (0, 1, 6, 7, 0)[j // 2] if j < CHUNKS - 1 else 1
 
         def finish(j):
-            b = 2 + j % 4
-            back = bank[6 + (j // 2) % 2]
+            b = 2 + j % 6
+            back = bank[back_bank(j)]
             turn(ga, j, b)
             dat = keep.tile([P, H], BF16, name=f"dat{j}")
             nc.vector.tensor_tensor(
@@ -172,10 +207,10 @@ def tile_moe_sdb_silu_kernel(
             dst = da_bf[e - e % 2][:, (e % 2) * 4 * C : (e % 2 + 1) * 4 * C].bitcast(F32)
             nc.scalar.copy(
                 dst.rearrange("p (j s u) -> p j s u", j=2, u=2)[:, lo:hi],
-                bank[6 + e % 2][:].rearrange("p (j u s) -> p j s u", j=2, u=2)[:, lo:hi],
+                bank[back_bank(2 * e + lo)][:].rearrange("p (j u s) -> p j s u", j=2, u=2)[:, lo:hi],
             )
 
-        dx_banks = (0, 1, 2, 3, 4, 5, 6, 7, 0, 1, 2, 3)
+        dx_banks = (2, 3, 4, 3, 5, 6, 4, 7, 0, 1, 2, 5)
         dx = [rows.tile([P, S], F32, name=f"dx{kb}", tag="rows") for kb in range(4)]
 
         def product(kb, g):
@@ -183,10 +218,14 @@ def tile_moe_sdb_silu_kernel(
             b = dx_banks[3 * kb + g]
             for e in range(lo // C, hi // C):
                 d0, dk = e - e % 2, (e % 2) * C
+                if e < 4:
+                    codes, scales, col = w1_codes[kb], w1_scales[kb], e * P
+                else:
+                    codes, scales, col = last_codes, last_scales, kb * P
                 nc.tensor.matmul_mx(
                     out=bank[b][:, e * C - lo : (e + 1) * C - lo],
-                    lhsT=w1_codes[kb][:, e * P : (e + 1) * P].bitcast(FP8X4),
-                    lhsT_scale=w1_scales[kb][:, e * P : (e + 1) * P],
+                    lhsT=codes[:, col : col + P].bitcast(FP8X4),
+                    lhsT_scale=scales[:, col : col + P],
                     rhs=da_codes[d0][:, dk : dk + C].bitcast(FP8X4),
                     rhs_scale=da_scales[d0][:, dk : dk + C],
                     start=True,
@@ -197,59 +236,72 @@ def tile_moe_sdb_silu_kernel(
         first = {}
 
         def fetch(kb):
-            first[kb] = ring.tile([P, T], F32, name="first")
-            nc.vector.tensor_copy(first[kb][:], dx[kb][:].indirect(pos1_sb[:]))
+            first[kb] = keep.tile([P, T], F32, name=f"first{kb}", align_bytes=64)
+            for lo, hi in HALVES:
+                nc.vector.tensor_copy(first[kb][:, lo:hi], dx[kb][:].indirect(pos1_sb[:, lo // 16 : hi // 16]))
 
         def combine(kb):
-            if kb in (1, 2):
-                both = w1_bf[kb + 1][:, E * 512 - 2 * T :].bitcast(F32)
+            if kb == 1:
+                both = da_bf[4][:].bitcast(F32)
+            elif kb == 2:
+                both = first[1]
             else:
                 both = ring.tile([P, T], F32, name="both")
-            cuts = ((0, T),) if kb < 3 else ((0, 416), (416, T))
-            for lo, hi in cuts:
+            for lo, hi in HALVES:
                 nc.vector.tensor_tensor(
                     both[:, lo:hi], dx[kb][:].indirect(pos2_sb[:, lo // 16 : hi // 16]), first[kb][:, lo:hi], ALU.add
                 )
-                nc.sync.dma_start(out[kb * P : (kb + 1) * P, lo:hi], both[:, lo:hi])
+                if kb == 3:
+                    nc.sync.dma_start(out[kb * P : (kb + 1) * P, lo:hi], both[:, lo:hi])
+            if kb < 3:
+                nc.sync.dma_start(out[kb * P : (kb + 1) * P, :], both[:, 0:T])
 
         for j in range(2):
             factor(j)
+        cast_w1(0, 0)
+        cast_w1(0, 1)
         for j in range(CHUNKS):
             finish(j)
             if j + 2 < CHUNKS:
                 factor(j + 2)
+            if j == 3:
+                cast_w1(1, 0)
+            if j == 5:
+                cast_w1(2, 0)
             if j % 2 == 1 and j < 8:
-                e = j // 2
-                cast_w1(e // 3, e % 3)
-                unturn(e)
+                unturn(j // 2)
             if j >= 8:
                 unturn(4, j - 8, j - 7)
+        quantize_w1(0, 0, 4)
         quantize_da(0)
-        for lo, hi in GROUPS:
-            quantize_w1(0, lo, hi)
         quantize_da(2)
         quantize_da(4)
-        cast_w1(1, 1)
         for g in range(3):
             product(0, g)
-        cast_w1(1, 2)
-        for lo, hi in GROUPS:
-            quantize_w1(1, lo, hi)
-        cast_w1(2, 2)
+        quantize_w1(1, 0, 2)
+        quantize_w1(2, 0, 2)
+        cast_w1(1, 1)
+        product(1, 0)
+        product(1, 2)
         fetch(0)
-        cast_w1(2, 0)
-        for g in range(3):
-            product(1, g)
-        cast_w1(2, 1)
+        quantize_w1(1, 2, 4)
+        product(1, 1)
         combine(0)
-        for kb in (2, 3):
-            if kb == 3:
-                for g in range(3):
-                    cast_w1(3, g)
-            fetch(kb - 1)
-            for g in (0, 2, 1):
-                quantize_w1(kb, *PAIRS[g])
-                product(kb, g)
-            combine(kb - 1)
+        cast_w1(2, 1)
+        product(2, 0)
+        product(2, 2)
+        cast_w1(3, 0)
+        fetch(1)
+        quantize_w1(2, 2, 4)
+        product(2, 1)
+        combine(1)
+        quantize_w1(3, 0, 2)
+        cast_w1(3, 1)
+        product(3, 0)
+        product(3, 2)
+        fetch(2)
+        quantize_w1(3, 2, 4)
+        product(3, 1)
+        combine(2)
         fetch(3)
         combine(3)

@@ -119,8 +119,8 @@ def tile_moe_sdb_silu_kernel(
         for h in range(2):
             last_bf = keep.tile([P, 1024], BF16, name=f"lastbf{h}", align_bytes=64)
             nc.vector.tensor_copy(
-                last_bf[:].rearrange("p (c i t) -> p c t i", i=4, t=4),
-                w1_last[h][:].rearrange("p t (c i) -> p c t i", i=4),
+                last_bf[:].rearrange("p (k t) -> p k t", t=4),
+                w1_last[h][:].rearrange("p t k -> p k t"),
             )
             nc.vector.quantize_mx(
                 out=last_codes[:, 256 * h : 256 * (h + 1)].bitcast(FP8X4),
@@ -163,7 +163,10 @@ def tile_moe_sdb_silu_kernel(
             dst = staged(kb, g).rearrange("p (e c i t) -> p e c t i", e=hi - lo, i=4, t=4)
             src = w1_raw[g][:, :, :, P * kb : P * (kb + 1)].rearrange("p e t (c i) -> p e c t i", i=4)
             if (kb, g) in VECTOR_CASTS:
-                nc.vector.tensor_copy(dst, src)
+                nc.vector.tensor_copy(
+                    staged(kb, g).rearrange("p (e k t) -> p e k t", e=2, t=4),
+                    w1_raw[g][:, :, :, P * kb : P * (kb + 1)].rearrange("p e t k -> p e k t"),
+                )
             else:
                 nc.scalar.copy(dst, src)
 

@@ -19,16 +19,20 @@ FP4X4 = mybir.dt.float4_e2m1fn_x4
 ALU = mybir.AluOpType
 ACT = mybir.ActivationFunctionType
 
-PIECES = ((0, 512), (512, 1024), (1024, 1280))
+PACK = 4
+BANK = 512
+BANKS = 8
+BLOCKS = 4
 CHUNKS = S // P
-VECTOR_CASTS = ((1, 1),)
-AFTER_LAST = ((1, 1),)
-GATE_AT = 3
-HALVES = ((0, 384), (384, T))
+LAST = E - 1
+GROUPS = ((0, 2), (2, 4), (LAST, E))
+STAGE = 2 * P * PACK
 WINDOW = S + 32
-FIRST = ((0, 512), (512, S))
-GROUPS = ((0, 4), (4, 5))
-PAIRS = ((0, 2), (2, 4), (4, 5))
+GATHER_CUTS = (((0, 512), (512, S)), ((0, S),), ((0, S),), ((0, 6 * P), (6 * P, S)))
+PARTS = ((0, 384), (384, T))
+GATE_CHUNK = 3
+BACK_BANKS = (0, 1, 6, 7, 0)
+DX_BANKS = ((2, 3, 4), (3, 5, 6), (4, 7, 0), (1, 2, 5))
 
 
 def tile_moe_sdb_silu_kernel(
@@ -37,274 +41,268 @@ def tile_moe_sdb_silu_kernel(
     nc = tc.nc
     with ExitStack() as ctx:
         keep = ctx.enter_context(tc.tile_pool(name="keep", bufs=1))
-        ring = ctx.enter_context(tc.tile_pool(name="ring", bufs=3))
-        rows = ctx.enter_context(tc.tile_pool(name="rows", bufs=4))
+        sums = ctx.enter_context(tc.tile_pool(name="sums", bufs=3))
+        rows = ctx.enter_context(tc.tile_pool(name="rows", bufs=BLOCKS))
         psum = ctx.enter_context(tc.psum_pool(name="psum", bufs=1))
-        bank = [psum.tile([P, 512], F32, name=f"bank{b}") for b in range(8)]
+        bank = [psum.tile([P, BANK], F32, name=f"bank{b}") for b in range(BANKS)]
 
-        planes = keep.tile([P, T + H], U8, align_bytes=64)
-        nc.gpsimd.memset(planes[:].bitcast(I32), 0)
-        warm = keep.tile([P, 8], F32)
-        warm2 = keep.tile([P, 8], F32)
-        nc.vector.memset(warm[:], 0.0)
-        nc.scalar.activation(warm2[:, 0:1], warm[:, 0:1], ACT.Sigmoid)
+        in_scales = keep.tile([P, T + H], U8, align_bytes=64)
+        nc.gpsimd.memset(in_scales[:].bitcast(I32), 0)
 
         dy_sb = keep.tile([P, T], U32, align_bytes=64)
         nc.sync.dma_start(dy_sb[:].bitcast(I32), dy_words[0].rearrange("p t d -> p (t d)").bitcast(I32))
         w2_sb = keep.tile([P, 2 * H], U8, align_bytes=64)
         nc.sync.dma_start(w2_sb[:].bitcast(I32), w2t_words[0].bitcast(I32))
-        a_sb = [rows.tile([P, S], F32, name=f"a{c}", tag="rows") for c in range(4)]
-        w1_last = [keep.tile([P, 4, 256], F32, name=f"w1last{h}") for h in range(2)]
+        a_sb = [rows.tile([P, S], F32, name=f"a{c}", tag="rows") for c in range(BLOCKS)]
+        last_raw = [keep.tile([P, PACK, K // 2], F32, name=f"lastraw{h}") for h in range(2)]
         for r in range(4):
-            nc.sync.dma_start(planes[r:P:32, 0:T].bitcast(I32), dy_scales[0, r:16:4, :].bitcast(I32))
-            nc.sync.dma_start(planes[r:P:32, T : T + H].bitcast(I32), w2t_scales[0, r:16:4, :].bitcast(I32))
+            nc.sync.dma_start(in_scales[r:P:32, 0:T].bitcast(I32), dy_scales[0, r:16:4, :].bitcast(I32))
+            nc.sync.dma_start(in_scales[r:P:32, T : T + H].bitcast(I32), w2t_scales[0, r:16:4, :].bitcast(I32))
             if r == 1:
                 for h in range(2):
-                    nc.sync.dma_start(
-                        w1_last[h][:], w1t[E - 1, :, 256 * h : 256 * (h + 1)].rearrange("(p j) k -> p j k", j=4)
-                    )
-        nc.sync.dma_start(a_sb[0][:, 0:512], a[0:P, 0:512])
+                    half = w1t[LAST, :, h * K // 2 : (h + 1) * K // 2]
+                    nc.sync.dma_start(last_raw[h][:], half.rearrange("(p t) k -> p t k", t=PACK))
+        cut = GATHER_CUTS[0][0][1]
+        nc.sync.dma_start(a_sb[0][:, 0:cut], a[0:P, 0:cut])
         offs_sb = keep.tile([P, S // 16], U16)
         nc.sync.dma_start(offs_sb[:], offs)
-        nc.sync.dma_start(a_sb[0][:, 512:S], a[0:P, 512:S])
-        for c in range(1, 4):
+        nc.sync.dma_start(a_sb[0][:, cut:S], a[0:P, cut:S])
+        for c in range(1, BLOCKS):
             nc.sync.dma_start(a_sb[c][:], a[c * P : (c + 1) * P, :])
         gate_rows = keep.tile([P, P], F32)
         nc.gpsimd.memset(gate_rows[:], 0.0)
         ident = keep.tile([P, P], F32)
         make_identity(nc, ident[:])
-        nc.sync.dma_start(gate_rows[0:CHUNKS, :], gate[0].rearrange("(c p) -> c p", p=P))
-        w1_raw = [keep.tile([P, hi - lo, 4, K], F32, name=f"w1raw{lo}") for lo, hi in PAIRS[:2]]
-        for g, (lo, hi) in enumerate(PAIRS[:2]):
-            nc.sync.dma_start(w1_raw[g][:], w1t[lo:hi].rearrange("e (p j) k -> p e j k", j=4))
+        nc.sync.dma_start(gate_rows[0:CHUNKS, :], gate[0].rearrange("(j p) -> j p", p=P))
+        pair_raw = [keep.tile([P, 2, PACK, K], F32, name=f"pairraw{g}") for g in range(2)]
+        for g in range(2):
+            lo, hi = GROUPS[g]
+            nc.sync.dma_start(pair_raw[g][:], w1t[lo:hi].rearrange("e (p t) k -> p e t k", t=PACK))
         pos1_sb = keep.tile([P, T // 16], U16)
         nc.sync.dma_start(pos1_sb[:], pos1)
         pos2_sb = keep.tile([P, T // 16], U16)
         nc.sync.dma_start(pos2_sb[:], pos2)
 
-        dc = [keep.tile([P, WINDOW], F32, name=f"dc{c}") for c in range(4)]
-        for c in range(4):
+        dc = [keep.tile([P, WINDOW], F32, name=f"dc{c}") for c in range(BLOCKS)]
+        for c in range(BLOCKS):
             nc.vector.memset(dc[c][:, T:WINDOW], 0.0)
-        sg = [keep.tile([P, S], F32, name=f"sg{c}") for c in range(4)]
-        ga = [keep.tile([P, S], F32, name=f"ga{c}") for c in range(4)]
-        for c in range(4):
-            cuts = ((c, 0, 0, 512), (4 + c, 0, 512, T)) if c else ((0, 0, 0, 256), (4, 0, 256, 512), (4, 256, 512, T))
-            for b, at, lo, hi in cuts:
+        sigm = [keep.tile([P, S], F32, name=f"sigm{c}") for c in range(BLOCKS)]
+        picked = [keep.tile([P, S], F32, name=f"picked{c}") for c in range(BLOCKS)]
+        split = (256, BANK, BANK, BANK)
+        for c in range(BLOCKS):
+            ends = sorted({0, split[c], BANK, T})
+            for lo, hi in zip(ends, ends[1:]):
+                b, col = (c, lo) if lo < split[c] else (BLOCKS + c, lo - split[c])
                 nc.tensor.matmul_mx(
-                    out=bank[b][:, at : at + hi - lo],
+                    out=bank[b][:, col : col + hi - lo],
                     lhsT=w2_sb[:, 2 * P * c : 2 * P * (c + 1)].bitcast(FP4X4),
-                    lhsT_scale=planes[:, T + P * c : T + P * (c + 1)],
+                    lhsT_scale=in_scales[:, T + P * c : T + P * (c + 1)],
                     rhs=dy_sb[:, lo:hi].bitcast(FP8X4),
-                    rhs_scale=planes[:, lo:hi],
+                    rhs_scale=in_scales[:, lo:hi],
                     start=True,
                     stop=True,
                 )
-        for c in range(4):
+        for c in range(BLOCKS):
             if c == 0:
-                for lo, hi in FIRST:
-                    nc.scalar.activation(sg[c][:, lo:hi], a_sb[c][:, lo:hi], ACT.Sigmoid)
-                nc.vector.tensor_copy(dc[c][:, 0:256], bank[c][:, 0:256])
-                nc.vector.tensor_copy(dc[c][:, 256:T], bank[4 + c][:, 0 : T - 256])
+                for lo, hi in GATHER_CUTS[0]:
+                    nc.scalar.activation(sigm[c][:, lo:hi], a_sb[c][:, lo:hi], ACT.Sigmoid)
+                nc.vector.tensor_copy(dc[c][:, 0 : split[c]], bank[c][:, 0 : split[c]])
+                nc.vector.tensor_copy(dc[c][:, split[c] : T], bank[BLOCKS + c][:, 0 : T - split[c]])
             else:
-                nc.scalar.copy(dc[c][:, 0:512], bank[c][:])
-                nc.scalar.copy(dc[c][:, 512:T], bank[4 + c][:, 0 : T - 512])
-                nc.scalar.activation(sg[c][:], a_sb[c][:], ACT.Sigmoid)
-            for lo, hi in (FIRST, ((0, S),), ((0, S),), ((0, 768), (768, S)))[c]:
+                nc.scalar.copy(dc[c][:, 0 : split[c]], bank[c][:])
+                nc.scalar.copy(dc[c][:, split[c] : T], bank[BLOCKS + c][:, 0 : T - split[c]])
+                nc.scalar.activation(sigm[c][:], a_sb[c][:], ACT.Sigmoid)
+            for lo, hi in GATHER_CUTS[c]:
                 nc.vector.tensor_tensor(
-                    ga[c][:, lo:hi], dc[c][:].indirect(offs_sb[:, lo // 16 : hi // 16]), sg[c][:, lo:hi], ALU.mult
+                    picked[c][:, lo:hi],
+                    dc[c][:].indirect(offs_sb[:, lo // 16 : hi // 16]),
+                    sigm[c][:, lo:hi],
+                    ALU.mult,
                 )
 
         last_codes = keep.tile([P, K], U32, align_bytes=64)
         last_scales = keep.tile([P, K], U8, align_bytes=64)
         for h in range(2):
-            last_bf = keep.tile([P, 1024], BF16, name=f"lastbf{h}", align_bytes=64)
+            last_bf = keep.tile([P, PACK * K // 2], BF16, name=f"lastbf{h}", align_bytes=64)
             nc.vector.tensor_copy(
-                last_bf[:].rearrange("p (k t) -> p k t", t=4),
-                w1_last[h][:].rearrange("p t k -> p k t"),
+                last_bf[:].rearrange("p (k t) -> p k t", t=PACK), last_raw[h][:].rearrange("p t k -> p k t")
             )
             nc.vector.quantize_mx(
-                out=last_codes[:, 256 * h : 256 * (h + 1)].bitcast(FP8X4),
-                scales=last_scales[:, 256 * h : 256 * (h + 1)],
+                out=last_codes[:, h * K // 2 : (h + 1) * K // 2].bitcast(FP8X4),
+                scales=last_scales[:, h * K // 2 : (h + 1) * K // 2],
                 in_=last_bf[:],
             )
 
         neg_gate = keep.tile([P, 16], F32)
 
-        def turn(src, j, b):
-            for c in range(4):
-                nc.tensor.transpose(bank[b][:, c * P : (c + 1) * P], src[c][:, j * P : (j + 1) * P], ident[:])
+        def turn(blocks, j, b):
+            spread = bank[b][:].rearrange("s (u p e) -> s p u e", u=2, e=2)
+            for c in range(BLOCKS):
+                nc.tensor.transpose(spread[:, 32 * c : 32 * (c + 1)], blocks[c][:, j * P : (j + 1) * P], ident[:])
 
-        def paired(b):
-            return bank[b][:].rearrange("s (p u e) -> s u p e", u=2, e=2)
-
-        yt = [keep.tile([P, H], F32, name=f"yt{j}") for j in range(CHUNKS)]
+        rest = [keep.tile([P, H], F32, name=f"rest{j}") for j in range(CHUNKS)]
         for j in range(CHUNKS):
-            turn(a_sb, j, j % 8)
-            nc.scalar.activation(
-                yt[j][:].rearrange("s (u p e) -> s u p e", u=2, e=2), paired(j % 8), ACT.Silu, scale=-1.0
-            )
-            if j == GATE_AT:
+            turn(a_sb, j, j % BANKS)
+            nc.scalar.activation(rest[j][:], bank[j % BANKS][:], ACT.Silu, scale=-1.0)
+            if j == GATE_CHUNK:
                 nc.tensor.transpose(bank[j][:, 0:P], gate_rows[:], ident[:])
                 nc.scalar.activation(neg_gate[:, 0:CHUNKS], bank[j][:, 0:CHUNKS], ACT.Copy, scale=-1.0)
 
-        w1_bf = [keep.tile([P, 2048 if kb == 0 else 1024], BF16, name=f"w1bf{kb}", align_bytes=64) for kb in range(3)]
-        w1_codes = [keep.tile([P, 4 * P], U32, name=f"w1codes{kb}", align_bytes=64) for kb in range(4)]
-        w1_scales = [keep.tile([P, 4 * P], U8, name=f"w1scales{kb}", align_bytes=64) for kb in range(4)]
+        own_stage = [
+            keep.tile([P, 2 * STAGE if kb == 0 else STAGE], BF16, name=f"stage{kb}", align_bytes=64)
+            for kb in range(BLOCKS - 1)
+        ]
+        pair_codes = [keep.tile([P, 4 * P], U32, name=f"paircodes{kb}", align_bytes=64) for kb in range(BLOCKS)]
+        pair_scales = [keep.tile([P, 4 * P], U8, name=f"pairscales{kb}", align_bytes=64) for kb in range(BLOCKS)]
 
         def staged(kb, g):
-            if kb == 3:
-                return first[g][:].bitcast(BF16)[:, 0:1024]
+            if kb == BLOCKS - 1:
+                return first[g][:].bitcast(BF16)[:, 0:STAGE]
             if kb > 0 and g == 1:
-                return da_bf[4][:, 0:1024]
-            return w1_bf[kb][:, g * 1024 : (g + 1) * 1024]
+                return da_bf[2][:, 0:STAGE]
+            return own_stage[kb][:, g * STAGE : (g + 1) * STAGE]
 
-        def cast_w1(kb, g):
-            lo, hi = PAIRS[g]
-            dst = staged(kb, g).rearrange("p (e c i t) -> p e c t i", e=hi - lo, i=4, t=4)
-            src = w1_raw[g][:, :, :, P * kb : P * (kb + 1)].rearrange("p e t (c i) -> p e c t i", i=4)
-            if (kb, g) in VECTOR_CASTS:
-                nc.vector.tensor_copy(
-                    staged(kb, g).rearrange("p (e k t) -> p e k t", e=2, t=4),
-                    w1_raw[g][:, :, :, P * kb : P * (kb + 1)].rearrange("p e t k -> p e k t"),
-                )
-            else:
-                nc.scalar.copy(dst, src)
-
-        def quantize_w1(kb, lo, hi):
-            nc.vector.quantize_mx(
-                out=w1_codes[kb][:, lo * P : hi * P].bitcast(FP8X4),
-                scales=w1_scales[kb][:, lo * P : hi * P],
-                in_=staged(kb, lo // 2) if hi - lo == 2 else w1_bf[kb][:],
+        def round_on_scalar(kb, g):
+            nc.scalar.copy(
+                staged(kb, g).rearrange("p (e c i t) -> p e c t i", e=2, i=4, t=PACK),
+                pair_raw[g][:, :, :, P * kb : P * (kb + 1)].rearrange("p e t (c i) -> p e c t i", i=4),
             )
 
-        def factor(j):
-            nc.vector.tensor_scalar(yt[j][:], yt[j][:], 1.0, neg_gate[:, j : j + 1], ALU.subtract, ALU.mult)
+        def round_on_vector(kb, g):
+            nc.vector.tensor_copy(
+                staged(kb, g).rearrange("p (e k t) -> p e k t", e=2, t=PACK),
+                pair_raw[g][:, :, :, P * kb : P * (kb + 1)].rearrange("p e t k -> p e k t"),
+            )
 
-        da_codes = {lo: keep.tile([P, (hi - lo) * C], U32, name=f"dacodes{lo}", align_bytes=64) for lo, hi in PAIRS}
-        da_scales = {lo: keep.tile([P, (hi - lo) * C], U8, name=f"dascales{lo}", align_bytes=64) for lo, hi in PAIRS}
-        da_bf = {lo: keep.tile([P, max((hi - lo) * 4 * C, 2 * T)], BF16, name=f"dabf{lo}", align_bytes=64) for lo, hi in PAIRS}
+        def quantize_weights(kb, lo, hi, rounded):
+            nc.vector.quantize_mx(
+                out=pair_codes[kb][:, lo * P : hi * P].bitcast(FP8X4),
+                scales=pair_scales[kb][:, lo * P : hi * P],
+                in_=rounded,
+            )
 
-        def quantize_da(lo):
-            nc.vector.quantize_mx(out=da_codes[lo][:].bitcast(FP8X4), scales=da_scales[lo][:], in_=da_bf[lo][:, 0 : 1024 if lo == 4 else 2048])
+        def quantize_pair(kb, g):
+            quantize_weights(kb, *GROUPS[g], staged(kb, g))
+
+        def gate_rest(j):
+            nc.vector.tensor_scalar(rest[j][:], rest[j][:], 1.0, neg_gate[:, j : j + 1], ALU.subtract, ALU.mult)
+
+        widths = [(hi - lo) * C for lo, hi in GROUPS]
+        da_codes = [keep.tile([P, n], U32, name=f"dacodes{g}", align_bytes=64) for g, n in enumerate(widths)]
+        da_scales = [keep.tile([P, n], U8, name=f"dascales{g}", align_bytes=64) for g, n in enumerate(widths)]
+        da_bf = [
+            keep.tile([P, max(PACK * n, 2 * T)], BF16, name=f"dabf{g}", align_bytes=64) for g, n in enumerate(widths)
+        ]
+
+        def quantize_da(g):
+            nc.vector.quantize_mx(
+                out=da_codes[g][:].bitcast(FP8X4), scales=da_scales[g][:], in_=da_bf[g][:, 0 : PACK * widths[g]]
+            )
 
         def back_bank(j):
-            return (0, 1, 6, 7, 0)[j // 2] if j < CHUNKS - 1 else 1
+            return bank[BACK_BANKS[j // 2] if j < CHUNKS - 1 else 1]
 
-        def finish(j):
+        def finish_chunk(j):
             b = 2 + j % 6
-            back = bank[back_bank(j)]
-            turn(ga, j, b)
-            dat = keep.tile([P, H], BF16, name=f"dat{j}")
-            nc.vector.tensor_tensor(
-                dat[:].rearrange("s (u p e) -> s u p e", u=2, e=2),
-                paired(b),
-                yt[j][:].rearrange("s (u p e) -> s u p e", u=2, e=2),
-                ALU.mult,
-            )
-            words = dat[:].bitcast(F32)
+            turn(picked, j, b)
+            da_turned = keep.tile([P, H], BF16, name=f"daturned{j}")
+            nc.vector.tensor_tensor(da_turned[:], bank[b][:], rest[j][:], ALU.mult)
+            words = da_turned[:].bitcast(F32)
             for u in range(2):
-                q = 2 * (j % 2) + u
-                nc.tensor.transpose(back[:, q * P : (q + 1) * P], words[:, u * P : (u + 1) * P], ident[:])
+                col = (2 * (j % 2) + u) * P
+                nc.tensor.transpose(back_bank(j)[:, col : col + P], words[:, u * P : (u + 1) * P], ident[:])
 
-        def unturn(e, lo=0, hi=2):
-            dst = da_bf[e - e % 2][:, (e % 2) * 4 * C : (e % 2 + 1) * 4 * C].bitcast(F32)
+        def collect_words(j, count):
+            e, jj = divmod(j, 2)
+            dst = da_bf[e // 2][:, (e % 2) * PACK * C : (e % 2 + 1) * PACK * C].bitcast(F32)
             nc.scalar.copy(
-                dst.rearrange("p (j s u) -> p j s u", j=2, u=2)[:, lo:hi],
-                bank[back_bank(2 * e + lo)][:].rearrange("p (j u s) -> p j s u", j=2, u=2)[:, lo:hi],
+                dst.rearrange("p (j s u) -> p j s u", j=2, u=2)[:, jj : jj + count],
+                back_bank(j)[:].rearrange("p (j u s) -> p j s u", j=2, u=2)[:, jj : jj + count],
             )
 
-        dx_banks = (2, 3, 4, 3, 5, 6, 4, 7, 0, 1, 2, 5)
-        dx = [rows.tile([P, S], F32, name=f"dx{kb}", tag="rows") for kb in range(4)]
+        dx = [rows.tile([P, S], F32, name=f"dx{kb}", tag="rows") for kb in range(BLOCKS)]
 
         def product(kb, g):
-            lo, hi = PIECES[g]
-            b = dx_banks[3 * kb + g]
-            for e in range(lo // C, hi // C):
-                d0, dk = e - e % 2, (e % 2) * C
-                if e < 4:
-                    codes, scales, col = w1_codes[kb], w1_scales[kb], e * P
+            lo, hi = GROUPS[g]
+            acc = bank[DX_BANKS[kb][g]]
+            for e in range(lo, hi):
+                col = (e - lo) * C
+                if e == LAST:
+                    codes, scales, w0 = last_codes, last_scales, kb * P
                 else:
-                    codes, scales, col = last_codes, last_scales, kb * P
+                    codes, scales, w0 = pair_codes[kb], pair_scales[kb], e * P
                 nc.tensor.matmul_mx(
-                    out=bank[b][:, e * C - lo : (e + 1) * C - lo],
-                    lhsT=codes[:, col : col + P].bitcast(FP8X4),
-                    lhsT_scale=scales[:, col : col + P],
-                    rhs=da_codes[d0][:, dk : dk + C].bitcast(FP8X4),
-                    rhs_scale=da_scales[d0][:, dk : dk + C],
+                    out=acc[:, col : col + C],
+                    lhsT=codes[:, w0 : w0 + P].bitcast(FP8X4),
+                    lhsT_scale=scales[:, w0 : w0 + P],
+                    rhs=da_codes[g][:, col : col + C].bitcast(FP8X4),
+                    rhs_scale=da_scales[g][:, col : col + C],
                     start=True,
                     stop=True,
                 )
-            nc.scalar.copy(dx[kb][:, lo:hi], bank[b][:, 0 : hi - lo])
+            nc.scalar.copy(dx[kb][:, lo * C : hi * C], acc[:, 0 : widths[g]])
 
         first = {}
 
-        def fetch(kb):
+        def fetch_first(kb):
             first[kb] = keep.tile([P, T], F32, name=f"first{kb}", align_bytes=64)
-            for lo, hi in HALVES:
+            for lo, hi in PARTS:
                 nc.vector.tensor_copy(first[kb][:, lo:hi], dx[kb][:].indirect(pos1_sb[:, lo // 16 : hi // 16]))
 
-        def combine(kb):
+        def add_second(kb):
             if kb == 1:
-                both = da_bf[4][:].bitcast(F32)
+                both = da_bf[2][:].bitcast(F32)
             elif kb == 2:
                 both = first[1]
             else:
-                both = ring.tile([P, T], F32, name="both")
-            for lo, hi in HALVES:
+                both = sums.tile([P, T], F32, name="both")
+            at_end = kb == BLOCKS - 1
+            for lo, hi in PARTS:
                 nc.vector.tensor_tensor(
                     both[:, lo:hi], dx[kb][:].indirect(pos2_sb[:, lo // 16 : hi // 16]), first[kb][:, lo:hi], ALU.add
                 )
-                if kb == 3:
+                if at_end:
                     nc.sync.dma_start(out[kb * P : (kb + 1) * P, lo:hi], both[:, lo:hi])
-            if kb < 3:
+            if not at_end:
                 nc.sync.dma_start(out[kb * P : (kb + 1) * P, :], both[:, 0:T])
 
         for j in range(2):
-            factor(j)
-        cast_w1(0, 0)
-        cast_w1(0, 1)
+            gate_rest(j)
+        round_on_scalar(0, 0)
+        round_on_scalar(1, 0)
+        rounds_after = {3: (2, 0), 5: (0, 1)}
         for j in range(CHUNKS):
-            finish(j)
+            finish_chunk(j)
             if j + 2 < CHUNKS:
-                factor(j + 2)
-            if j == 3:
-                cast_w1(1, 0)
-            if j == 5:
-                cast_w1(2, 0)
-            if j % 2 == 1 and j < 8:
-                unturn(j // 2)
-            if j >= 8:
-                unturn(4, j - 8, j - 7)
-        quantize_w1(0, 0, 4)
-        quantize_da(0)
-        quantize_da(2)
-        quantize_da(4)
-        for g in range(3):
+                gate_rest(j + 2)
+            if j in rounds_after:
+                round_on_scalar(*rounds_after[j])
+            if j // 2 == LAST:
+                collect_words(j, 1)
+            elif j % 2 == 1:
+                collect_words(j - 1, 2)
+        quantize_weights(0, 0, LAST, own_stage[0][:])
+        for g in range(len(GROUPS)):
+            quantize_da(g)
+        for g in range(len(GROUPS)):
             product(0, g)
-        quantize_w1(1, 0, 2)
-        quantize_w1(2, 0, 2)
-        cast_w1(1, 1)
-        product(1, 0)
-        product(1, 2)
-        fetch(0)
-        quantize_w1(1, 2, 4)
-        product(1, 1)
-        combine(0)
-        cast_w1(2, 1)
-        product(2, 0)
-        product(2, 2)
-        cast_w1(3, 0)
-        fetch(1)
-        quantize_w1(2, 2, 4)
-        product(2, 1)
-        combine(1)
-        quantize_w1(3, 0, 2)
-        cast_w1(3, 1)
-        product(3, 0)
-        product(3, 2)
-        fetch(2)
-        quantize_w1(3, 2, 4)
-        product(3, 1)
-        combine(2)
-        fetch(3)
-        combine(3)
+
+        quantize_pair(1, 0)
+        quantize_pair(2, 0)
+        for kb in range(1, BLOCKS):
+            if kb == 1:
+                round_on_vector(kb, 1)
+            else:
+                if kb == BLOCKS - 1:
+                    quantize_pair(kb, 0)
+                round_on_scalar(kb, 1)
+            product(kb, 0)
+            product(kb, 2)
+            if kb == BLOCKS - 2:
+                round_on_scalar(kb + 1, 0)
+            fetch_first(kb - 1)
+            quantize_pair(kb, 1)
+            product(kb, 1)
+            add_second(kb - 1)
+        fetch_first(BLOCKS - 1)
+        add_second(BLOCKS - 1)

from contextlib import ExitStack

import concourse.mybir as mybir
from concourse.masks import make_identity

K, T, E, C, H, N = 512, 640, 5, 256, 512, 512
S = E * C
P = 128
FLOPS = 2 * N * H * T + 2 * H * K * S

F32 = mybir.dt.float32
BF16 = mybir.dt.bfloat16
I32 = mybir.dt.int32
U32 = mybir.dt.uint32
U16 = mybir.dt.uint16
U8 = mybir.dt.uint8
FP8X4 = mybir.dt.float8_e4m3fn_x4
FP4X4 = mybir.dt.float4_e2m1fn_x4
ALU = mybir.AluOpType
ACT = mybir.ActivationFunctionType

PACK = 4
BANK = 512
BANKS = 8
BLOCKS = 4
CHUNKS = S // P
LAST = E - 1
GROUPS = ((0, 2), (2, 4), (LAST, E))
STAGE = 2 * P * PACK
WINDOW = S + 32
GATHER_CUTS = (((0, 512), (512, S)), ((0, S),), ((0, S),), ((0, 6 * P), (6 * P, S)))
PARTS = ((0, 384), (384, T))
GATE_CHUNK = 3
BACK_BANKS = (0, 1, 6, 7, 0)
DX_BANKS = ((2, 3, 4), (3, 5, 6), (4, 7, 0), (1, 2, 5))


def tile_moe_sdb_silu_kernel(
    tc, dy_words, dy_scales, w2t_words, w2t_scales, w1t, a, gate, offs, pos1, pos2, out
):
    nc = tc.nc
    with ExitStack() as ctx:
        keep = ctx.enter_context(tc.tile_pool(name="keep", bufs=1))
        sums = ctx.enter_context(tc.tile_pool(name="sums", bufs=3))
        rows = ctx.enter_context(tc.tile_pool(name="rows", bufs=BLOCKS))
        psum = ctx.enter_context(tc.psum_pool(name="psum", bufs=1))
        bank = [psum.tile([P, BANK], F32, name=f"bank{b}") for b in range(BANKS)]

        in_scales = keep.tile([P, T + H], U8, align_bytes=64)
        nc.gpsimd.memset(in_scales[:].bitcast(I32), 0)

        dy_sb = keep.tile([P, T], U32, align_bytes=64)
        nc.sync.dma_start(dy_sb[:].bitcast(I32), dy_words[0].rearrange("p t d -> p (t d)").bitcast(I32))
        w2_sb = keep.tile([P, 2 * H], U8, align_bytes=64)
        nc.sync.dma_start(w2_sb[:].bitcast(I32), w2t_words[0].bitcast(I32))
        a_sb = [rows.tile([P, S], F32, name=f"a{c}", tag="rows") for c in range(BLOCKS)]
        last_raw = [keep.tile([P, PACK, K // 2], F32, name=f"lastraw{h}") for h in range(2)]
        for r in range(4):
            nc.sync.dma_start(in_scales[r:P:32, 0:T].bitcast(I32), dy_scales[0, r:16:4, :].bitcast(I32))
            nc.sync.dma_start(in_scales[r:P:32, T : T + H].bitcast(I32), w2t_scales[0, r:16:4, :].bitcast(I32))
            if r == 1:
                for h in range(2):
                    half = w1t[LAST, :, h * K // 2 : (h + 1) * K // 2]
                    nc.sync.dma_start(last_raw[h][:], half.rearrange("(p t) k -> p t k", t=PACK))
        cut = GATHER_CUTS[0][0][1]
        nc.sync.dma_start(a_sb[0][:, 0:cut], a[0:P, 0:cut])
        offs_sb = keep.tile([P, S // 16], U16)
        nc.sync.dma_start(offs_sb[:], offs)
        nc.sync.dma_start(a_sb[0][:, cut:S], a[0:P, cut:S])
        for c in range(1, BLOCKS):
            nc.sync.dma_start(a_sb[c][:], a[c * P : (c + 1) * P, :])
        gate_rows = keep.tile([P, P], F32)
        nc.gpsimd.memset(gate_rows[:], 0.0)
        ident = keep.tile([P, P], F32)
        make_identity(nc, ident[:])
        nc.sync.dma_start(gate_rows[0:CHUNKS, :], gate[0].rearrange("(j p) -> j p", p=P))
        pair_raw = [keep.tile([P, 2, PACK, K], F32, name=f"pairraw{g}") for g in range(2)]
        for g in range(2):
            lo, hi = GROUPS[g]
            nc.sync.dma_start(pair_raw[g][:], w1t[lo:hi].rearrange("e (p t) k -> p e t k", t=PACK))
        pos1_sb = keep.tile([P, T // 16], U16)
        nc.sync.dma_start(pos1_sb[:], pos1)
        pos2_sb = keep.tile([P, T // 16], U16)
        nc.sync.dma_start(pos2_sb[:], pos2)

        dc = [keep.tile([P, WINDOW], F32, name=f"dc{c}") for c in range(BLOCKS)]
        for c in range(BLOCKS):
            nc.vector.memset(dc[c][:, T:WINDOW], 0.0)
        sigm = [keep.tile([P, S], F32, name=f"sigm{c}") for c in range(BLOCKS)]
        picked = [keep.tile([P, S], F32, name=f"picked{c}") for c in range(BLOCKS)]
        split = (256, BANK, BANK, BANK)
        for c in range(BLOCKS):
            ends = sorted({0, split[c], BANK, T})
            for lo, hi in zip(ends, ends[1:]):
                b, col = (c, lo) if lo < split[c] else (BLOCKS + c, lo - split[c])
                nc.tensor.matmul_mx(
                    out=bank[b][:, col : col + hi - lo],
                    lhsT=w2_sb[:, 2 * P * c : 2 * P * (c + 1)].bitcast(FP4X4),
                    lhsT_scale=in_scales[:, T + P * c : T + P * (c + 1)],
                    rhs=dy_sb[:, lo:hi].bitcast(FP8X4),
                    rhs_scale=in_scales[:, lo:hi],
                    start=True,
                    stop=True,
                )
        for c in range(BLOCKS):
            if c == 0:
                for lo, hi in GATHER_CUTS[0]:
                    nc.scalar.activation(sigm[c][:, lo:hi], a_sb[c][:, lo:hi], ACT.Sigmoid)
                nc.vector.tensor_copy(dc[c][:, 0 : split[c]], bank[c][:, 0 : split[c]])
                nc.vector.tensor_copy(dc[c][:, split[c] : T], bank[BLOCKS + c][:, 0 : T - split[c]])
            else:
                nc.scalar.copy(dc[c][:, 0 : split[c]], bank[c][:])
                nc.scalar.copy(dc[c][:, split[c] : T], bank[BLOCKS + c][:, 0 : T - split[c]])
                nc.scalar.activation(sigm[c][:], a_sb[c][:], ACT.Sigmoid)
            for lo, hi in GATHER_CUTS[c]:
                nc.vector.tensor_tensor(
                    picked[c][:, lo:hi],
                    dc[c][:].indirect(offs_sb[:, lo // 16 : hi // 16]),
                    sigm[c][:, lo:hi],
                    ALU.mult,
                )

        last_codes = keep.tile([P, K], U32, align_bytes=64)
        last_scales = keep.tile([P, K], U8, align_bytes=64)
        for h in range(2):
            last_bf = keep.tile([P, PACK * K // 2], BF16, name=f"lastbf{h}", align_bytes=64)
            nc.vector.tensor_copy(
                last_bf[:].rearrange("p (k t) -> p k t", t=PACK), last_raw[h][:].rearrange("p t k -> p k t")
            )
            nc.vector.quantize_mx(
                out=last_codes[:, h * K // 2 : (h + 1) * K // 2].bitcast(FP8X4),
                scales=last_scales[:, h * K // 2 : (h + 1) * K // 2],
                in_=last_bf[:],
            )

        neg_gate = keep.tile([P, 16], F32)

        def turn(blocks, j, b):
            spread = bank[b][:].rearrange("s (u p e) -> s p u e", u=2, e=2)
            for c in range(BLOCKS):
                nc.tensor.transpose(spread[:, 32 * c : 32 * (c + 1)], blocks[c][:, j * P : (j + 1) * P], ident[:])

        rest = [keep.tile([P, H], F32, name=f"rest{j}") for j in range(CHUNKS)]
        for j in range(CHUNKS):
            turn(a_sb, j, j % BANKS)
            nc.scalar.activation(rest[j][:], bank[j % BANKS][:], ACT.Silu, scale=-1.0)
            if j == GATE_CHUNK:
                nc.tensor.transpose(bank[j][:, 0:P], gate_rows[:], ident[:])
                nc.scalar.activation(neg_gate[:, 0:CHUNKS], bank[j][:, 0:CHUNKS], ACT.Copy, scale=-1.0)

        own_stage = [
            keep.tile([P, 2 * STAGE if kb == 0 else STAGE], BF16, name=f"stage{kb}", align_bytes=64)
            for kb in range(BLOCKS - 1)
        ]
        pair_codes = [keep.tile([P, 4 * P], U32, name=f"paircodes{kb}", align_bytes=64) for kb in range(BLOCKS)]
        pair_scales = [keep.tile([P, 4 * P], U8, name=f"pairscales{kb}", align_bytes=64) for kb in range(BLOCKS)]

        def staged(kb, g):
            if kb == BLOCKS - 1:
                return first[g][:].bitcast(BF16)[:, 0:STAGE]
            if kb > 0 and g == 1:
                return da_bf[2][:, 0:STAGE]
            return own_stage[kb][:, g * STAGE : (g + 1) * STAGE]

        def round_on_scalar(kb, g):
            nc.scalar.copy(
                staged(kb, g).rearrange("p (e c i t) -> p e c t i", e=2, i=4, t=PACK),
                pair_raw[g][:, :, :, P * kb : P * (kb + 1)].rearrange("p e t (c i) -> p e c t i", i=4),
            )

        def round_on_vector(kb, g):
            nc.vector.tensor_copy(
                staged(kb, g).rearrange("p (e k t) -> p e k t", e=2, t=PACK),
                pair_raw[g][:, :, :, P * kb : P * (kb + 1)].rearrange("p e t k -> p e k t"),
            )

        def quantize_weights(kb, lo, hi, rounded):
            nc.vector.quantize_mx(
                out=pair_codes[kb][:, lo * P : hi * P].bitcast(FP8X4),
                scales=pair_scales[kb][:, lo * P : hi * P],
                in_=rounded,
            )

        def quantize_pair(kb, g):
            quantize_weights(kb, *GROUPS[g], staged(kb, g))

        def gate_rest(j):
            nc.vector.tensor_scalar(rest[j][:], rest[j][:], 1.0, neg_gate[:, j : j + 1], ALU.subtract, ALU.mult)

        widths = [(hi - lo) * C for lo, hi in GROUPS]
        da_codes = [keep.tile([P, n], U32, name=f"dacodes{g}", align_bytes=64) for g, n in enumerate(widths)]
        da_scales = [keep.tile([P, n], U8, name=f"dascales{g}", align_bytes=64) for g, n in enumerate(widths)]
        da_bf = [
            keep.tile([P, max(PACK * n, 2 * T)], BF16, name=f"dabf{g}", align_bytes=64) for g, n in enumerate(widths)
        ]

        def quantize_da(g):
            nc.vector.quantize_mx(
                out=da_codes[g][:].bitcast(FP8X4), scales=da_scales[g][:], in_=da_bf[g][:, 0 : PACK * widths[g]]
            )

        def back_bank(j):
            return bank[BACK_BANKS[j // 2] if j < CHUNKS - 1 else 1]

        def finish_chunk(j):
            b = 2 + j % 6
            turn(picked, j, b)
            da_turned = keep.tile([P, H], BF16, name=f"daturned{j}")
            nc.vector.tensor_tensor(da_turned[:], bank[b][:], rest[j][:], ALU.mult)
            words = da_turned[:].bitcast(F32)
            for u in range(2):
                col = (2 * (j % 2) + u) * P
                nc.tensor.transpose(back_bank(j)[:, col : col + P], words[:, u * P : (u + 1) * P], ident[:])

        def collect_words(j, count):
            e, jj = divmod(j, 2)
            dst = da_bf[e // 2][:, (e % 2) * PACK * C : (e % 2 + 1) * PACK * C].bitcast(F32)
            nc.scalar.copy(
                dst.rearrange("p (j s u) -> p j s u", j=2, u=2)[:, jj : jj + count],
                back_bank(j)[:].rearrange("p (j u s) -> p j s u", j=2, u=2)[:, jj : jj + count],
            )

        dx = [rows.tile([P, S], F32, name=f"dx{kb}", tag="rows") for kb in range(BLOCKS)]

        def product(kb, g):
            lo, hi = GROUPS[g]
            acc = bank[DX_BANKS[kb][g]]
            for e in range(lo, hi):
                col = (e - lo) * C
                if e == LAST:
                    codes, scales, w0 = last_codes, last_scales, kb * P
                else:
                    codes, scales, w0 = pair_codes[kb], pair_scales[kb], e * P
                nc.tensor.matmul_mx(
                    out=acc[:, col : col + C],
                    lhsT=codes[:, w0 : w0 + P].bitcast(FP8X4),
                    lhsT_scale=scales[:, w0 : w0 + P],
                    rhs=da_codes[g][:, col : col + C].bitcast(FP8X4),
                    rhs_scale=da_scales[g][:, col : col + C],
                    start=True,
                    stop=True,
                )
            nc.scalar.copy(dx[kb][:, lo * C : hi * C], acc[:, 0 : widths[g]])

        first = {}

        def fetch_first(kb):
            first[kb] = keep.tile([P, T], F32, name=f"first{kb}", align_bytes=64)
            for lo, hi in PARTS:
                nc.vector.tensor_copy(first[kb][:, lo:hi], dx[kb][:].indirect(pos1_sb[:, lo // 16 : hi // 16]))

        def add_second(kb):
            if kb == 1:
                both = da_bf[2][:].bitcast(F32)
            elif kb == 2:
                both = first[1]
            else:
                both = sums.tile([P, T], F32, name="both")
            at_end = kb == BLOCKS - 1
            for lo, hi in PARTS:
                nc.vector.tensor_tensor(
                    both[:, lo:hi], dx[kb][:].indirect(pos2_sb[:, lo // 16 : hi // 16]), first[kb][:, lo:hi], ALU.add
                )
                if at_end:
                    nc.sync.dma_start(out[kb * P : (kb + 1) * P, lo:hi], both[:, lo:hi])
            if not at_end:
                nc.sync.dma_start(out[kb * P : (kb + 1) * P, :], both[:, 0:T])

        for j in range(2):
            gate_rest(j)
        round_on_scalar(0, 0)
        round_on_scalar(1, 0)
        rounds_after = {3: (2, 0), 5: (0, 1)}
        for j in range(CHUNKS):
            finish_chunk(j)
            if j + 2 < CHUNKS:
                gate_rest(j + 2)
            if j in rounds_after:
                round_on_scalar(*rounds_after[j])
            if j // 2 == LAST:
                collect_words(j, 1)
            elif j % 2 == 1:
                collect_words(j - 1, 2)
        quantize_weights(0, 0, LAST, own_stage[0][:])
        for g in range(len(GROUPS)):
            quantize_da(g)
        for g in range(len(GROUPS)):
            product(0, g)

        quantize_pair(1, 0)
        quantize_pair(2, 0)
        for kb in range(1, BLOCKS):
            if kb == 1:
                round_on_vector(kb, 1)
            else:
                if kb == BLOCKS - 1:
                    quantize_pair(kb, 0)
                round_on_scalar(kb, 1)
            product(kb, 0)
            product(kb, 2)
            if kb == BLOCKS - 2:
                round_on_scalar(kb + 1, 0)
            fetch_first(kb - 1)
            quantize_pair(kb, 1)
            product(kb, 1)
            add_second(kb - 1)
        fetch_first(BLOCKS - 1)
        add_second(BLOCKS - 1)
